import numpy as np
import ml_dtypes


def mxq(x, axis, fmt="e4m3"):
    dtype, down = {"e4m3": (ml_dtypes.float8_e4m3fn, 7), "e5m2": (ml_dtypes.float8_e5m2, 14)}[fmt]
    v = np.moveaxis(np.asarray(x, np.float32).astype(ml_dtypes.bfloat16).astype(np.float64), axis, -1)
    blocks = v.reshape(v.shape[:-1] + (-1, 32))
    amax = np.abs(blocks).max(-1, keepdims=True)
    byte = np.maximum(np.where(amax > 0, np.frexp(amax)[1] - 1 + 127, 0) - down, 1)
    scale = np.exp2(byte - 127.0)
    codes = (blocks / scale).astype(np.float32).astype(dtype).astype(np.float64)
    return np.moveaxis((codes * scale).reshape(v.shape), -1, axis)


WIDE = False


def mx_kscale(k):
    if not WIDE:
        return np.ones(k)
    levels = np.array([10, -10, 5, -5, 0])
    if k % 512:
        return np.exp2(np.random.permutation(np.resize(levels, k // 32))).repeat(32)
    a = np.empty((k // 512, 16))
    for p in range(k // 512):
        a[p, :8] = np.random.permutation(np.resize(levels, 8))
        for g in range(8):
            far = levels[np.abs(levels - a[p, g]) >= 10]
            a[p, g + 8] = far[np.random.randint(len(far))]
    return np.exp2(a.ravel()).repeat(32)


def f64(x):
    return np.asarray(x).astype(np.float64)


def striped8(idx):
    return np.asarray(idx).reshape(8, -1, 16).transpose(0, 2, 1).reshape(128, -1).astype(np.uint16)


def unstriped8(offs):
    return offs.reshape(8, 16, -1).transpose(0, 2, 1).reshape(8, -1).astype(np.int64)


def pick8(x, idx, run):
    r = np.arange(len(x))
    return x[r[:, None], idx[r % (8 * run) // run]]


E2M1 = np.array([0.0, 0.5, 1.0, 1.5, 2.0, 3.0, 4.0, 6.0, -0.0, -0.5, -1.0, -1.5, -2.0, -3.0, -4.0, -6.0])


def pack_weight(w, fmt):
    k, n = w.shape
    w = f64(np.asarray(w, np.float32).astype(ml_dtypes.bfloat16)).reshape(k // 32, 32, n)
    amax = np.abs(w).max(1)
    if fmt == "e4m3":
        byte = np.frexp(amax)[1] - 1 + 127 - 7
    else:
        mant, ex = np.frexp(amax / 6.0)
        byte = np.where(mant > 0.5, ex, ex - 1) + 127
    byte = np.clip(np.where(amax > 0, byte, 1), 1, 254)
    scaled = (w * np.exp2(127.0 - byte)[:, None, :]).reshape(k, n).astype(np.float32)
    by_word = np.ascontiguousarray(scaled.reshape(k // 512, 128, 4, n).transpose(0, 1, 3, 2))
    if fmt == "e4m3":
        words = by_word.astype(ml_dtypes.float8_e4m3fn).view(np.uint8)
    else:
        c = by_word.astype(ml_dtypes.float4_e2m1fn).view(np.uint8) & 0xF
        words = (c[..., 0::2] | (c[..., 1::2] << 4)).reshape(k // 512, 128, 2 * n)
    return np.ascontiguousarray(words), np.ascontiguousarray(byte.astype(np.uint8).reshape(k // 512, 16, n))


def unpack_weight(words, scales, fmt):
    g, _, n = scales.shape
    words = np.ascontiguousarray(words).reshape(g, 128, n, -1)
    if fmt == "e4m3":
        vals = words.view(ml_dtypes.float8_e4m3fn).astype(np.float64)
    else:
        nib = np.empty((g, 128, n, 4), np.uint8)
        nib[..., 0::2] = words & 0xF
        nib[..., 1::2] = words >> 4
        vals = E2M1[nib]
    vals = vals * np.repeat(np.exp2(scales.astype(np.float64) - 127.0), 8, axis=1)[..., None]
    return vals.transpose(0, 1, 3, 2).reshape(g * 512, n)


D, K, T, U, I, Q = 512, 512, 1024, 1024, 512, 128


def setup_inputs():
    n = np.random.standard_normal
    idx = np.stack([np.random.permutation(T)[:I] for _ in range(8)])
    idx2 = np.stack([np.random.permutation(T)[:I] for _ in range(8)])
    idx3 = np.stack([np.random.permutation(U)[:I] for _ in range(8)])
    idx4 = np.stack([np.random.permutation(U)[:I] for _ in range(8)])
    idx5 = np.stack([np.random.permutation(T)[:I] for _ in range(8)])
    fd = mx_kscale(D)
    fk = mx_kscale(K)
    wqp = pack_weight(n((D, K)) * 1.0 / np.sqrt(D) * fd[:, None] * fk, "e4m3")
    cachep = pack_weight(n((K, T)) * 1.0 / np.sqrt(K) / fk[:, None], "e4m3")
    draftp = pack_weight(n((D, U)) * 1.0 / np.sqrt(D) * fd[:, None], "e2m1")
    return {
        "states": (n((D, Q)) * 0.95 / fd[:, None]).astype(np.float32),
        "wq_words": wqp[0],
        "wq_scales": wqp[1],
        "cache_words": cachep[0],
        "cache_scales": cachep[1],
        "draft_words": draftp[0],
        "draft_scales": draftp[1],
        "offs": striped8(idx),
        "offs2": striped8(idx2),
        "offs3": striped8(idx3),
        "offs4": striped8(idx4),
        "offs5": striped8(idx5),
    }


def reference(states, wq_words, wq_scales, cache_words, cache_scales, draft_words, draft_scales, offs, offs2, offs3, offs4, offs5):
    idx = unstriped8(offs)
    idx2 = unstriped8(offs2)
    idx3 = unstriped8(offs3)
    idx4 = unstriped8(offs4)
    idx5 = unstriped8(offs5)
    wqu = unpack_weight(wq_words, wq_scales, "e4m3")
    cacheu = unpack_weight(cache_words, cache_scales, "e4m3")
    draftu = unpack_weight(draft_words, draft_scales, "e2m1")
    statesq = mxq(f64(states), 0, "e4m3")
    qv = wqu.T @ statesq
    qvq = mxq(qv, 0, "e4m3")
    a = qvq.T @ cacheu
    b = statesq.T @ draftu
    lo1 = np.minimum(pick8(a, idx, 16), pick8(a, idx2, 16))
    hi1 = np.maximum(pick8(a, idx, 16), pick8(a, idx2, 16))
    f1 = np.zeros((Q, U))
    f1[np.arange(Q)[:, None], idx3[np.arange(Q) % 128 // 16]] = lo1
    bb = np.maximum(b, f1)
    v = pick8(bb, idx4, 16) - hi1
    f2 = np.zeros((Q, T))
    f2[np.arange(Q)[:, None], idx5[np.arange(Q) % 128 // 16]] = v
    aa = a + f2
    y = pick8(aa, idx2, 16)
    return y

@@ -1,0 +1,161 @@
+from contextlib import ExitStack
+
+import concourse.mybir as mybir
+
+F32 = mybir.dt.float32
+BF16 = mybir.dt.bfloat16
+I32 = mybir.dt.int32
+U32 = mybir.dt.uint32
+U16 = mybir.dt.uint16
+U8 = mybir.dt.uint8
+FP8X4 = mybir.dt.float8_e4m3fn_x4
+FP4X4 = mybir.dt.float4_e2m1fn_x4
+ALU = mybir.AluOpType
+COPY = mybir.ActivationFunctionType.Copy
+
+P = 128
+PACK = 4
+D, K, T, U, I, Q = 512, 512, 1024, 1024, 512, 128
+FLOPS = 2 * (D * K * Q + K * Q * T + D * Q * U)
+HALF = I // 2
+A_WIDTHS = (256, 256, 256, 128, 128)
+B_COLS = 512
+
+
+def load_scales(queue, plane, scales):
+    for r in range(4):
+        queue.dma_start(out=plane[r:P:32, :].bitcast(I32), in_=scales[0, r:16:4, :].bitcast(I32))
+
+
+def tile_attend_evictlow_side_kernel(tc, states, wq_words, wq_scales, cache_words, cache_scales, draft_words, draft_scales, offs, offs2, offs3, offs4, offs5, out):
+    nc = tc.nc
+    with ExitStack() as ctx:
+        sb = ctx.enter_context(tc.tile_pool(name="sb", bufs=1))
+        ps = ctx.enter_context(tc.psum_pool(name="ps", bufs=1))
+
+        wq_plane_raw = sb.tile([P, K], U8, align_bytes=64)
+        cache_plane = sb.tile([P, T], U8, align_bytes=64)
+        draft_plane = sb.tile([P, U], U8, align_bytes=64)
+        nc.gpsimd.memset(wq_plane_raw[:].bitcast(U32), 0)
+        nc.gpsimd.memset(cache_plane[:].bitcast(U32), 0)
+        nc.gpsimd.memset(draft_plane[:].bitcast(U32), 0)
+        f1 = sb.tile([P, U], F32)
+        nc.vector.memset(f1[:], 0.0)
+
+        st_raw = sb.tile([P, PACK, Q], F32)
+        wq_raw = sb.tile([P, K], I32)
+        cache_w = sb.tile([P, T], I32, align_bytes=64)
+        draft_w = sb.tile([P, 2 * U], U8, align_bytes=64)
+        lists = [sb.tile([P, I // 16], U16, name=f"list{n}") for n in range(5)]
+
+        nc.sync.dma_start(out=st_raw[:], in_=states.rearrange("(p j) q -> p j q", j=PACK))
+        load_scales(nc.scalar, wq_plane_raw, wq_scales)
+        nc.sync.dma_start(out=wq_raw[:], in_=wq_words[0].rearrange("p n t -> p (n t)").bitcast(I32))
+        nc.sync.dma_start(out=cache_w[:], in_=cache_words[0].rearrange("p n t -> p (n t)").bitcast(I32))
+        load_scales(nc.sync, cache_plane, cache_scales)
+        nc.sync.dma_start(lists[0][:], offs)
+        nc.sync.dma_start(lists[1][:], offs2)
+        nc.sync.dma_start(out=draft_w[:].bitcast(I32), in_=draft_words[0].bitcast(I32))
+        load_scales(nc.sync, draft_plane, draft_scales)
+        nc.sync.dma_start(lists[2][:], offs3)
+        nc.sync.dma_start(lists[3][:], offs4)
+        nc.sync.dma_start(lists[4][:], offs5)
+
+        def half_list(n, h):
+            return lists[n][:, h * HALF // 16 : (h + 1) * HALF // 16]
+
+        halves = [slice(h * HALF, (h + 1) * HALF) for h in range(2)]
+
+        st_bf = sb.tile([P, Q * PACK], BF16, align_bytes=64)
+        st_out = st_bf[:].rearrange("p (c i t) -> p c t i", t=PACK, i=4)
+        st_in = st_raw[:].rearrange("p t (c i) -> p c t i", i=4)
+        nc.vector.tensor_copy(out=st_out, in_=st_in)
+        wq_plane = sb.tile([P, K], U8, align_bytes=64)
+        nc.vector.tensor_copy(
+            out=wq_plane[:].rearrange("p (t c i) -> p c t i", t=PACK, i=16),
+            in_=wq_plane_raw[:].rearrange("p (c i t) -> p c t i", t=PACK, i=16),
+        )
+
+        st_codes = sb.tile([P, Q], U32, align_bytes=64)
+        st_plane = sb.tile([P, Q], U8, align_bytes=64)
+        nc.vector.quantize_mx(out=st_codes[:].bitcast(FP8X4), scales=st_plane[:], in_=st_bf[:])
+
+        wq_w = [sb.tile([P, 2 * P], U32, name=f"wq_w{n}", align_bytes=64) for n in range(2)]
+        wq_by_place = wq_raw[:].bitcast(U32).rearrange("p (c i t) -> p c t i", t=PACK, i=4)
+        nc.vector.tensor_copy(out=wq_w[0][:].bitcast(I32).rearrange("p (t c i) -> p c t i", t=2, i=4), in_=wq_raw[:].rearrange("p (c i t) -> p c t i", t=PACK, i=4)[:, :, 0:2, :])
+        nc.scalar.copy(out=wq_w[1][:].rearrange("p (t c i) -> p c t i", t=2, i=4), in_=wq_by_place[:, :, 2:4, :])
+
+        qv_ps = ps.tile([P, PACK, Q], F32)
+        for t in range(PACK):
+            nc.tensor.matmul_mx(
+                out=qv_ps[:, t, :],
+                lhsT=wq_w[t // 2][:, (t % 2) * P : (t % 2 + 1) * P].bitcast(FP8X4),
+                lhsT_scale=wq_plane[:, t * P : (t + 1) * P],
+                rhs=st_codes[:].bitcast(FP8X4),
+                rhs_scale=st_plane[:],
+                start=True,
+                stop=True,
+            )
+        qv_bf = sb.tile([P, Q, PACK], BF16, align_bytes=64)
+        nc.scalar.copy(out=qv_bf[:], in_=qv_ps[:].rearrange("p t q -> p q t"))
+        qv_codes = sb.tile([P, Q], U32, align_bytes=64)
+        qv_plane = sb.tile([P, Q], U8, align_bytes=64)
+        nc.vector.quantize_mx(out=qv_codes[:].bitcast(FP8X4), scales=qv_plane[:], in_=qv_bf[:].rearrange("p q t -> p (q t)"))
+
+        a = sb.tile([P, T], F32)
+        for n, width in enumerate(A_WIDTHS):
+            first = sum(A_WIDTHS[:n])
+            cols = slice(first, first + width)
+            a_ps = ps.tile([P, width], F32, name=f"a_ps{n}")
+            nc.tensor.matmul_mx(
+                out=a_ps[:], lhsT=qv_codes[:].bitcast(FP8X4), lhsT_scale=qv_plane[:],
+                rhs=cache_w[:, cols].bitcast(FP8X4), rhs_scale=cache_plane[:, cols], start=True, stop=True,
+            )
+            if n % 2 == 0:
+                nc.scalar.copy(out=a[:, cols], in_=a_ps[:])
+            else:
+                nc.vector.tensor_copy(out=a[:, cols], in_=a_ps[:])
+
+        b_ps = [ps.tile([P, B_COLS], F32, name=f"b_ps{n}") for n in range(U // B_COLS)]
+        for n in range(U // B_COLS):
+            nc.tensor.matmul_mx(
+                out=b_ps[n][:], lhsT=st_codes[:].bitcast(FP8X4), lhsT_scale=st_plane[:],
+                rhs=draft_w[:, 2 * n * B_COLS : 2 * (n + 1) * B_COLS].bitcast(FP4X4),
+                rhs_scale=draft_plane[:, n * B_COLS : (n + 1) * B_COLS], start=True, stop=True,
+            )
+
+        g2 = [sb.tile([P, HALF], F32, name=f"g2_{h}", tag=f"second{h}") for h in range(2)]
+        lo = [sb.tile([P, HALF], F32, name=f"lo_{h}") for h in range(2)]
+        hi = [sb.tile([P, HALF], F32, name=f"hi_{h}") for h in range(2)]
+        for h in range(2):
+            g1 = sb.tile([P, HALF], F32, name=f"g1_{h}", tag="first")
+            nc.vector.tensor_copy(g1[:], a[:].indirect(half_list(0, h)))
+            nc.scalar.activation(g2[h][:], a[:].indirect(half_list(1, h)), COPY)
+            nc.vector.tensor_tensor(lo[h][:], g1[:], g2[h][:], ALU.min)
+            nc.vector.tensor_tensor(hi[h][:], g1[:], g2[h][:], ALU.max)
+        for h in range(2):
+            nc.scalar.activation(f1[:].indirect(half_list(2, h)), lo[h][:], COPY)
+        f2 = [sb.tile([P, T], F32, name="f2_0", tag="first"), sb.tile([P, T], F32, name="f2_1", tag="second1")]
+        for h in range(2):
+            nc.vector.memset(f2[h][:], 0.0)
+
+        bb = sb.tile([P, U], F32)
+        for n in range(U // B_COLS):
+            cols = slice(n * B_COLS, (n + 1) * B_COLS)
+            nc.vector.tensor_tensor(bb[:, cols], b_ps[n][:], f1[:, cols], ALU.max)
+
+        v = [sb.tile([P, HALF], F32, name=f"v_{h}") for h in range(2)]
+        for h in range(2):
+            nc.vector.tensor_tensor(v[h][:], bb[:].indirect(half_list(3, h)), hi[h][:], ALU.subtract)
+            nc.scalar.activation(f2[h][:].indirect(half_list(4, h)), v[h][:], COPY)
+
+        a_part = sb.tile([P, T], F32)
+        aa = sb.tile([P, T], F32)
+        nc.vector.tensor_tensor(a_part[:], a[:], f2[0][:], ALU.add)
+        nc.vector.tensor_tensor(aa[:], a_part[:], f2[1][:], ALU.add)
+
+        y = [sb.tile([P, HALF], F32, name=f"y_{h}") for h in range(2)]
+        nc.vector.tensor_copy(y[0][:], aa[:].indirect(half_list(1, 0)))
+        nc.scalar.activation(y[1][:], aa[:].indirect(half_list(1, 1)), COPY)
+        nc.sync.dma_start(out=out[:, halves[0]], in_=y[0][:])
+        nc.scalar.dma_start(out=out[:, halves[1]], in_=y[1][:])

@@ -20,11 +20,12 @@ FLOPS = 2 * (D * K * Q + K * Q * T + D * Q * U)
 HALF = I // 2
 A_WIDTHS = (256, 256, 256, 128, 128)
 B_COLS = 512
+CAST_SPLIT = 20
 
 
-def load_scales(queue, plane, scales):
+def load_scales(queues, plane, scales):
     for r in range(4):
-        queue.dma_start(out=plane[r:P:32, :].bitcast(I32), in_=scales[0, r:16:4, :].bitcast(I32))
+        queues[r % len(queues)].dma_start(out=plane[r:P:32, :].bitcast(I32), in_=scales[0, r:16:4, :].bitcast(I32))
 
 
 def tile_attend_evictlow_side_kernel(tc, states, wq_words, wq_scales, cache_words, cache_scales, draft_words, draft_scales, offs, offs2, offs3, offs4, offs5, out):
@@ -37,10 +38,12 @@ def tile_attend_evictlow_side_kernel(tc, states, wq_words, wq_scales, cache_word
         cache_plane = sb.tile([P, T], U8, align_bytes=64)
         draft_plane = sb.tile([P, U], U8, align_bytes=64)
         nc.gpsimd.memset(wq_plane_raw[:].bitcast(U32), 0)
-        nc.gpsimd.memset(cache_plane[:].bitcast(U32), 0)
-        nc.gpsimd.memset(draft_plane[:].bitcast(U32), 0)
+        nc.vector.memset(cache_plane[:].bitcast(U32), 0)
+        nc.vector.memset(draft_plane[:].bitcast(U32), 0)
         f1 = sb.tile([P, U], F32)
         nc.vector.memset(f1[:], 0.0)
+        f2_early = sb.tile([P, T], F32)
+        nc.vector.memset(f2_early[:], 0.0)
 
         st_raw = sb.tile([P, PACK, Q], F32)
         wq_raw = sb.tile([P, K], I32)
@@ -49,14 +52,14 @@ def tile_attend_evictlow_side_kernel(tc, states, wq_words, wq_scales, cache_word
         lists = [sb.tile([P, I // 16], U16, name=f"list{n}") for n in range(5)]
 
         nc.sync.dma_start(out=st_raw[:], in_=states.rearrange("(p j) q -> p j q", j=PACK))
-        load_scales(nc.scalar, wq_plane_raw, wq_scales)
+        load_scales((nc.scalar, nc.sync), wq_plane_raw, wq_scales)
         nc.sync.dma_start(out=wq_raw[:], in_=wq_words[0].rearrange("p n t -> p (n t)").bitcast(I32))
         nc.sync.dma_start(out=cache_w[:], in_=cache_words[0].rearrange("p n t -> p (n t)").bitcast(I32))
-        load_scales(nc.sync, cache_plane, cache_scales)
+        load_scales((nc.sync,), cache_plane, cache_scales)
         nc.sync.dma_start(lists[0][:], offs)
         nc.sync.dma_start(lists[1][:], offs2)
         nc.sync.dma_start(out=draft_w[:].bitcast(I32), in_=draft_words[0].bitcast(I32))
-        load_scales(nc.sync, draft_plane, draft_scales)
+        load_scales((nc.sync,), draft_plane, draft_scales)
         nc.sync.dma_start(lists[2][:], offs3)
         nc.sync.dma_start(lists[3][:], offs4)
         nc.sync.dma_start(lists[4][:], offs5)
@@ -69,7 +72,8 @@ def tile_attend_evictlow_side_kernel(tc, states, wq_words, wq_scales, cache_word
         st_bf = sb.tile([P, Q * PACK], BF16, align_bytes=64)
         st_out = st_bf[:].rearrange("p (c i t) -> p c t i", t=PACK, i=4)
         st_in = st_raw[:].rearrange("p t (c i) -> p c t i", i=4)
-        nc.vector.tensor_copy(out=st_out, in_=st_in)
+        nc.vector.tensor_copy(out=st_out[:, 0:CAST_SPLIT], in_=st_in[:, 0:CAST_SPLIT])
+        nc.scalar.copy(out=st_out[:, CAST_SPLIT:], in_=st_in[:, CAST_SPLIT:])
         wq_plane = sb.tile([P, K], U8, align_bytes=64)
         nc.vector.tensor_copy(
             out=wq_plane[:].rearrange("p (t c i) -> p c t i", t=PACK, i=16),
@@ -82,13 +86,13 @@ def tile_attend_evictlow_side_kernel(tc, states, wq_words, wq_scales, cache_word
 
         wq_w = [sb.tile([P, 2 * P], U32, name=f"wq_w{n}", align_bytes=64) for n in range(2)]
         wq_by_place = wq_raw[:].bitcast(U32).rearrange("p (c i t) -> p c t i", t=PACK, i=4)
-        nc.vector.tensor_copy(out=wq_w[0][:].bitcast(I32).rearrange("p (t c i) -> p c t i", t=2, i=4), in_=wq_raw[:].rearrange("p (c i t) -> p c t i", t=PACK, i=4)[:, :, 0:2, :])
-        nc.scalar.copy(out=wq_w[1][:].rearrange("p (t c i) -> p c t i", t=2, i=4), in_=wq_by_place[:, :, 2:4, :])
+        nc.vector.tensor_copy(out=wq_w[1][:].bitcast(I32).rearrange("p (t c i) -> p c t i", t=2, i=4), in_=wq_raw[:].rearrange("p (c i t) -> p c t i", t=PACK, i=4)[:, :, 2:4, :])
+        nc.scalar.copy(out=wq_w[0][:].rearrange("p (t c i) -> p c t i", t=2, i=4), in_=wq_by_place[:, :, 0:2, :])
 
-        qv_ps = ps.tile([P, PACK, Q], F32)
+        qv_ps = [ps.tile([P, 2, Q], F32, name=f"qv_ps{n}") for n in range(2)]
         for t in range(PACK):
             nc.tensor.matmul_mx(
-                out=qv_ps[:, t, :],
+                out=qv_ps[t // 2][:, t % 2, :],
                 lhsT=wq_w[t // 2][:, (t % 2) * P : (t % 2 + 1) * P].bitcast(FP8X4),
                 lhsT_scale=wq_plane[:, t * P : (t + 1) * P],
                 rhs=st_codes[:].bitcast(FP8X4),
@@ -97,7 +101,8 @@ def tile_attend_evictlow_side_kernel(tc, states, wq_words, wq_scales, cache_word
                 stop=True,
             )
         qv_bf = sb.tile([P, Q, PACK], BF16, align_bytes=64)
-        nc.scalar.copy(out=qv_bf[:], in_=qv_ps[:].rearrange("p t q -> p q t"))
+        nc.scalar.copy(out=qv_bf[:, :, 0:2], in_=qv_ps[0][:].rearrange("p t q -> p q t"))
+        nc.vector.tensor_copy(out=qv_bf[:, :, 2:4], in_=qv_ps[1][:].rearrange("p t q -> p q t"))
         qv_codes = sb.tile([P, Q], U32, align_bytes=64)
         qv_plane = sb.tile([P, Q], U8, align_bytes=64)
         nc.vector.quantize_mx(out=qv_codes[:].bitcast(FP8X4), scales=qv_plane[:], in_=qv_bf[:].rearrange("p q t -> p (q t)"))
@@ -116,7 +121,7 @@ def tile_attend_evictlow_side_kernel(tc, states, wq_words, wq_scales, cache_word
             else:
                 nc.vector.tensor_copy(out=a[:, cols], in_=a_ps[:])
 
-        b_ps = [ps.tile([P, B_COLS], F32, name=f"b_ps{n}") for n in range(U // B_COLS)]
+        b_ps = [ps.tile([P, B_COLS], F32, name=f"b_ps{n}", tag=f"a_ps{n}") for n in range(U // B_COLS)]
         for n in range(U // B_COLS):
             nc.tensor.matmul_mx(
                 out=b_ps[n][:], lhsT=st_codes[:].bitcast(FP8X4), lhsT_scale=st_plane[:],
@@ -135,9 +140,8 @@ def tile_attend_evictlow_side_kernel(tc, states, wq_words, wq_scales, cache_word
             nc.vector.tensor_tensor(hi[h][:], g1[:], g2[h][:], ALU.max)
         for h in range(2):
             nc.scalar.activation(f1[:].indirect(half_list(2, h)), lo[h][:], COPY)
-        f2 = [sb.tile([P, T], F32, name="f2_0", tag="first"), sb.tile([P, T], F32, name="f2_1", tag="second1")]
-        for h in range(2):
-            nc.vector.memset(f2[h][:], 0.0)
+        f2 = [sb.tile([P, T], F32, name="f2_0", tag="first"), f2_early]
+        nc.vector.memset(f2[0][:], 0.0)
 
         bb = sb.tile([P, U], F32)
         for n in range(U // B_COLS):

from contextlib import ExitStack

import concourse.mybir as mybir

F32 = mybir.dt.float32
BF16 = mybir.dt.bfloat16
I32 = mybir.dt.int32
U32 = mybir.dt.uint32
U16 = mybir.dt.uint16
U8 = mybir.dt.uint8
FP8X4 = mybir.dt.float8_e4m3fn_x4
FP4X4 = mybir.dt.float4_e2m1fn_x4
ALU = mybir.AluOpType
COPY = mybir.ActivationFunctionType.Copy

P = 128
PACK = 4
D, K, T, U, I, Q = 512, 512, 1024, 1024, 512, 128
FLOPS = 2 * (D * K * Q + K * Q * T + D * Q * U)
HALF = I // 2
A_WIDTHS = (256, 256, 256, 128, 128)
B_COLS = 512
CAST_SPLIT = 20


def load_scales(queues, plane, scales):
    for r in range(4):
        queues[r % len(queues)].dma_start(out=plane[r:P:32, :].bitcast(I32), in_=scales[0, r:16:4, :].bitcast(I32))


def tile_attend_evictlow_side_kernel(tc, states, wq_words, wq_scales, cache_words, cache_scales, draft_words, draft_scales, offs, offs2, offs3, offs4, offs5, out):
    nc = tc.nc
    with ExitStack() as ctx:
        sb = ctx.enter_context(tc.tile_pool(name="sb", bufs=1))
        ps = ctx.enter_context(tc.psum_pool(name="ps", bufs=1))

        wq_plane_raw = sb.tile([P, K], U8, align_bytes=64)
        cache_plane = sb.tile([P, T], U8, align_bytes=64)
        draft_plane = sb.tile([P, U], U8, align_bytes=64)
        nc.gpsimd.memset(wq_plane_raw[:].bitcast(U32), 0)
        nc.vector.memset(cache_plane[:].bitcast(U32), 0)
        nc.vector.memset(draft_plane[:].bitcast(U32), 0)
        f1 = sb.tile([P, U], F32)
        nc.vector.memset(f1[:], 0.0)
        f2_early = sb.tile([P, T], F32)
        nc.vector.memset(f2_early[:], 0.0)

        st_raw = sb.tile([P, PACK, Q], F32)
        wq_raw = sb.tile([P, K], I32)
        cache_w = sb.tile([P, T], I32, align_bytes=64)
        draft_w = sb.tile([P, 2 * U], U8, align_bytes=64)
        lists = [sb.tile([P, I // 16], U16, name=f"list{n}") for n in range(5)]

        nc.sync.dma_start(out=st_raw[:], in_=states.rearrange("(p j) q -> p j q", j=PACK))
        load_scales((nc.scalar, nc.sync), wq_plane_raw, wq_scales)
        nc.sync.dma_start(out=wq_raw[:], in_=wq_words[0].rearrange("p n t -> p (n t)").bitcast(I32))
        nc.sync.dma_start(out=cache_w[:], in_=cache_words[0].rearrange("p n t -> p (n t)").bitcast(I32))
        load_scales((nc.sync,), cache_plane, cache_scales)
        nc.sync.dma_start(lists[0][:], offs)
        nc.sync.dma_start(lists[1][:], offs2)
        nc.sync.dma_start(out=draft_w[:].bitcast(I32), in_=draft_words[0].bitcast(I32))
        load_scales((nc.sync,), draft_plane, draft_scales)
        nc.sync.dma_start(lists[2][:], offs3)
        nc.sync.dma_start(lists[3][:], offs4)
        nc.sync.dma_start(lists[4][:], offs5)

        def half_list(n, h):
            return lists[n][:, h * HALF // 16 : (h + 1) * HALF // 16]

        halves = [slice(h * HALF, (h + 1) * HALF) for h in range(2)]

        st_bf = sb.tile([P, Q * PACK], BF16, align_bytes=64)
        st_out = st_bf[:].rearrange("p (c i t) -> p c t i", t=PACK, i=4)
        st_in = st_raw[:].rearrange("p t (c i) -> p c t i", i=4)
        nc.vector.tensor_copy(out=st_out[:, 0:CAST_SPLIT], in_=st_in[:, 0:CAST_SPLIT])
        nc.scalar.copy(out=st_out[:, CAST_SPLIT:], in_=st_in[:, CAST_SPLIT:])
        wq_plane = sb.tile([P, K], U8, align_bytes=64)
        nc.vector.tensor_copy(
            out=wq_plane[:].rearrange("p (t c i) -> p c t i", t=PACK, i=16),
            in_=wq_plane_raw[:].rearrange("p (c i t) -> p c t i", t=PACK, i=16),
        )

        st_codes = sb.tile([P, Q], U32, align_bytes=64)
        st_plane = sb.tile([P, Q], U8, align_bytes=64)
        nc.vector.quantize_mx(out=st_codes[:].bitcast(FP8X4), scales=st_plane[:], in_=st_bf[:])

        wq_w = [sb.tile([P, 2 * P], U32, name=f"wq_w{n}", align_bytes=64) for n in range(2)]
        wq_by_place = wq_raw[:].bitcast(U32).rearrange("p (c i t) -> p c t i", t=PACK, i=4)
        nc.vector.tensor_copy(out=wq_w[1][:].bitcast(I32).rearrange("p (t c i) -> p c t i", t=2, i=4), in_=wq_raw[:].rearrange("p (c i t) -> p c t i", t=PACK, i=4)[:, :, 2:4, :])
        nc.scalar.copy(out=wq_w[0][:].rearrange("p (t c i) -> p c t i", t=2, i=4), in_=wq_by_place[:, :, 0:2, :])

        qv_ps = [ps.tile([P, 2, Q], F32, name=f"qv_ps{n}") for n in range(2)]
        for t in range(PACK):
            nc.tensor.matmul_mx(
                out=qv_ps[t // 2][:, t % 2, :],
                lhsT=wq_w[t // 2][:, (t % 2) * P : (t % 2 + 1) * P].bitcast(FP8X4),
                lhsT_scale=wq_plane[:, t * P : (t + 1) * P],
                rhs=st_codes[:].bitcast(FP8X4),
                rhs_scale=st_plane[:],
                start=True,
                stop=True,
            )
        qv_bf = sb.tile([P, Q, PACK], BF16, align_bytes=64)
        nc.scalar.copy(out=qv_bf[:, :, 0:2], in_=qv_ps[0][:].rearrange("p t q -> p q t"))
        nc.vector.tensor_copy(out=qv_bf[:, :, 2:4], in_=qv_ps[1][:].rearrange("p t q -> p q t"))
        qv_codes = sb.tile([P, Q], U32, align_bytes=64)
        qv_plane = sb.tile([P, Q], U8, align_bytes=64)
        nc.vector.quantize_mx(out=qv_codes[:].bitcast(FP8X4), scales=qv_plane[:], in_=qv_bf[:].rearrange("p q t -> p (q t)"))

        a = sb.tile([P, T], F32)
        for n, width in enumerate(A_WIDTHS):
            first = sum(A_WIDTHS[:n])
            cols = slice(first, first + width)
            a_ps = ps.tile([P, width], F32, name=f"a_ps{n}")
            nc.tensor.matmul_mx(
                out=a_ps[:], lhsT=qv_codes[:].bitcast(FP8X4), lhsT_scale=qv_plane[:],
                rhs=cache_w[:, cols].bitcast(FP8X4), rhs_scale=cache_plane[:, cols], start=True, stop=True,
            )
            if n % 2 == 0:
                nc.scalar.copy(out=a[:, cols], in_=a_ps[:])
            else:
                nc.vector.tensor_copy(out=a[:, cols], in_=a_ps[:])

        b_ps = [ps.tile([P, B_COLS], F32, name=f"b_ps{n}", tag=f"a_ps{n}") for n in range(U // B_COLS)]
        for n in range(U // B_COLS):
            nc.tensor.matmul_mx(
                out=b_ps[n][:], lhsT=st_codes[:].bitcast(FP8X4), lhsT_scale=st_plane[:],
                rhs=draft_w[:, 2 * n * B_COLS : 2 * (n + 1) * B_COLS].bitcast(FP4X4),
                rhs_scale=draft_plane[:, n * B_COLS : (n + 1) * B_COLS], start=True, stop=True,
            )

        g2 = [sb.tile([P, HALF], F32, name=f"g2_{h}", tag=f"second{h}") for h in range(2)]
        lo = [sb.tile([P, HALF], F32, name=f"lo_{h}") for h in range(2)]
        hi = [sb.tile([P, HALF], F32, name=f"hi_{h}") for h in range(2)]
        for h in range(2):
            g1 = sb.tile([P, HALF], F32, name=f"g1_{h}", tag="first")
            nc.vector.tensor_copy(g1[:], a[:].indirect(half_list(0, h)))
            nc.scalar.activation(g2[h][:], a[:].indirect(half_list(1, h)), COPY)
            nc.vector.tensor_tensor(lo[h][:], g1[:], g2[h][:], ALU.min)
            nc.vector.tensor_tensor(hi[h][:], g1[:], g2[h][:], ALU.max)
        for h in range(2):
            nc.scalar.activation(f1[:].indirect(half_list(2, h)), lo[h][:], COPY)
        f2 = [sb.tile([P, T], F32, name="f2_0", tag="first"), f2_early]
        nc.vector.memset(f2[0][:], 0.0)

        bb = sb.tile([P, U], F32)
        for n in range(U // B_COLS):
            cols = slice(n * B_COLS, (n + 1) * B_COLS)
            nc.vector.tensor_tensor(bb[:, cols], b_ps[n][:], f1[:, cols], ALU.max)

        v = [sb.tile([P, HALF], F32, name=f"v_{h}") for h in range(2)]
        for h in range(2):
            nc.vector.tensor_tensor(v[h][:], bb[:].indirect(half_list(3, h)), hi[h][:], ALU.subtract)
            nc.scalar.activation(f2[h][:].indirect(half_list(4, h)), v[h][:], COPY)

        a_part = sb.tile([P, T], F32)
        aa = sb.tile([P, T], F32)
        nc.vector.tensor_tensor(a_part[:], a[:], f2[0][:], ALU.add)
        nc.vector.tensor_tensor(aa[:], a_part[:], f2[1][:], ALU.add)

        y = [sb.tile([P, HALF], F32, name=f"y_{h}") for h in range(2)]
        nc.vector.tensor_copy(y[0][:], aa[:].indirect(half_list(1, 0)))
        nc.scalar.activation(y[1][:], aa[:].indirect(half_list(1, 1)), COPY)
        nc.sync.dma_start(out=out[:, halves[0]], in_=y[0][:])
        nc.scalar.dma_start(out=out[:, halves[1]], in_=y[1][:])
